import numpy as np
CORES = [88,96,104,112,120,216,224,232,240,248]
N = 10
W, KW = 128, 5
H = KW // 2
def setup_inputs(rng):
    return {"x": rng.standard_normal((N, 128, W), dtype=np.float32), "t": rng.standard_normal((N, 128, KW * W), dtype=np.float32)}
def setup_inputs_big(rng):
    d = setup_inputs(rng)
    for k in ("x", "t"): d[k] = (d[k].astype(np.float32) * 1024.0).astype(d[k].dtype)
    return d
def setup_inputs_small(rng):
    d = setup_inputs(rng)
    for k in ("x", "t"): d[k] = (d[k].astype(np.float32) * (1 / 1024.0)).astype(d[k].dtype)
    return d
def setup_inputs_apart(rng):
    d = setup_inputs(rng)
    f = (10.0 ** rng.permutation(np.linspace(-1.5, 1.5, N))).astype(np.float32).reshape(N, 1, 1)
    for k in ("x", "t"): d[k] = (d[k].astype(np.float32) * f).astype(d[k].dtype)
    return d
def reference(x, t):
    X, T = x.astype(np.float64), t.astype(np.float64)
    g = np.concatenate(list(X), axis=1)
    p = np.concatenate([g[:, -H:], g, g[:, :H]], axis=1)
    y = np.stack([sum(T[r][:, W * i:W * i + W] * p[:, W * r + i:W * r + i + W] for i in range(KW)) for r in range(N)])
    return {"y": y.astype(np.float32 if x.dtype != np.float64 else np.float64)}

@@ -1,0 +1,135 @@
+from concourse.bass import DstId, RemoteDMATransfer
+from concourse.mybir import AluOpType
+
+W = 128
+KW = 5
+H = 2
+
+SCRATCH = {
+    "edge": ("dram", [2, 128, H], "float32"),
+    "land": ("dram", [2, 128, H], "float32"),
+    "halo": ("sbuf", [128, 2 * H], "float32"),
+    "xs": ("sbuf", [128, W], "float32"),
+    "ts": ("sbuf", [128, KW * W], "float32"),
+    "xz": ("psum", [128, W + 2 * H], "float32"),
+    "pa": ("psum", [128, 2 * W], "float32"),
+    "pb": ("sbuf", [128, 2 * W], "float32"),
+    "pc": ("sbuf", [128, W], "float32"),
+    "u": ("sbuf", [128, W], "float32"),
+    "ys": ("sbuf", [128, W], "float32"),
+    "te": ("sbuf", [128, 2 * H], "float32"),
+    "q": ("sbuf", [128, 8], "float32"),
+}
+SEMAPHORES = ["cut", "xl", "tl", "relay", "sent", "arr0", "arr1", "hl", "vz", "vm", "va", "vg", "vh", "vi", "vj",
+              "vdone", "stored"]
+
+
+def _engines(allowed, n, busy=0):
+    m, bit = 0, 1
+    while n:
+        if allowed & bit and not busy & bit:
+            m |= bit
+            n -= 1
+        bit <<= 1
+    return m
+
+
+def _plan(T, topo):
+    cores = list(T.cores)
+    n = len(cores)
+    world = range((max(topo.host(c) for c in cores) + 1) * topo.CORES_PER_HOST)
+    ways = []
+    for r, c in enumerate(cores):
+        taken = []
+        for slot, step in ((0, 1), (1, -1)):
+            dst = cores[(r + step) % n]
+            via = None
+            if not topo.may_write(c, dst):
+                cand = [k for k in world
+                        if topo.host(k) == topo.host(c) and topo.chip(k) == topo.chip(c) and k not in cores
+                        and k not in taken and topo.may_write(k, dst)]
+                cand.sort(key=lambda k: (topo.die(k) != topo.die(c), k))
+                via = cand[0]
+                taken.append(via)
+            ways.append((c, slot, dst, via))
+    return ways
+
+
+def rank_program(g, core, T, topo):
+    S = T.sem
+    ways = _plan(T, topo)
+    arr = (S.arr0, S.arr1)
+
+    if T.rank_of(core) is None:
+        for (src, slot, dst, via) in ways:
+            if via == core:
+                rid, pid = topo.addr(dst, core)
+                g.wait_ge(S.relay, 1)
+                g.remote_dma(T.land[slot], T.edge[slot], arr[slot], S.sent, pid, rid,
+                             _engines(topo.mask(core, dst), 1))
+                g.wait_ge(S.sent, 1)
+        return
+
+    V, mult, add = g.vector, AluOpType.mult, AluOpType.add
+
+    g.sync.dma_start(T.edge[0], T.x[:, W - H:W]).then_inc(S.cut, 16)
+    g.scalar.dma_start(T.edge[1], T.x[:, 0:H]).then_inc(S.cut, 16)
+    g.scalar.dma_start(T.xs[:], T.x[:]).then_inc(S.xl, 16)
+    g.sync.dma_start(T.ts[:], T.t[:]).then_inc(S.tl, 16)
+
+    mine = [w for w in ways if w[0] == core]
+    g.wait_ge(S.cut, 32)
+    busy, trs = 0, []
+    for (src, slot, dst, via) in mine:
+        if via is not None:
+            rid, pid = topo.addr(via, core)
+            m = _engines(topo.mask(core, via), 1, busy)
+            busy |= m
+            trs.append(RemoteDMATransfer(dst_ids=[DstId(rid=rid, pnc=pid)], dma_engine_mask=m, remote_sem=S.relay,
+                                         src=T.edge[slot], dst=T.edge[slot]))
+    if trs:
+        g.remote_dma_fused(trs, local_sem=S.sent)
+    for (src, slot, dst, via) in mine:
+        if via is None:
+            rid, pid = topo.addr(dst, core)
+            g.remote_dma(T.land[slot], T.edge[slot], arr[slot], S.sent, pid, rid, _engines(topo.mask(core, dst), 1))
+    g.wait_ge(S.sent, len(mine))
+
+    g.sync.wait_ge(S.arr0, 1)
+    g.sync.dma_start(T.halo[:, 0:H], T.land[0]).then_inc(S.hl, 16)
+    g.scalar.wait_ge(S.arr1, 1)
+    g.scalar.dma_start(T.halo[:, H:2 * H], T.land[1]).then_inc(S.hl, 16)
+
+    V.memset(T.xz[:, 0:H], 0.0).then_inc(S.vz, 1)
+    V.memset(T.xz[:, W + H:W + 2 * H], 0.0).then_inc(S.vz, 1)
+    V.wait_ge(S.xl, 16)
+    V.tensor_copy(T.xz[:, H:W + H], T.xs[:]).then_inc(S.vz, 1)
+    V.wait_ge(S.tl, 16)
+    V.tensor_copy(T.te[:, 0:H], T.ts[:, 0:H]).then_inc(S.vg, 1)
+    V.tensor_copy(T.te[:, H:2 * H], T.ts[:, KW * W - H:KW * W]).then_inc(S.vg, 1)
+    V.wait_ge(S.vz, 3)
+    outs = (T.pa[:, 0:W], T.pa[:, W:2 * W], T.pb[:, 0:W], T.pb[:, W:2 * W], T.pc[:])
+    for i in range(KW):
+        V.tensor_tensor(out=outs[i], in0=T.ts[:, W * i:W * i + W], in1=T.xz[:, i:i + W], op=mult).then_inc(S.vm, 1)
+    V.wait_ge(S.vm, KW)
+    V.tensor_tensor(out=T.pa[:], in0=T.pa[:], in1=T.pb[:], op=add).then_inc(S.va, 1)
+    V.wait_ge(S.va, 1)
+    V.tensor_tensor(out=T.u[:], in0=T.pa[:, 0:W], in1=T.pc[:], op=add).then_inc(S.va, 1)
+    V.wait_ge(S.va, 2)
+    V.tensor_tensor(out=T.ys[:], in0=T.pa[:, W:2 * W], in1=T.u[:], op=add).then_inc(S.va, 1)
+    V.wait_ge(S.va, 3)
+    V.wait_ge(S.vg, 2)
+
+    V.wait_ge(S.hl, 32)
+    V.tensor_tensor(out=T.q[:, 0:4], in0=T.te[:], in1=T.halo[:], op=mult).then_inc(S.vh, 1)
+    V.tensor_tensor(out=T.q[:, 4:6], in0=T.ts[:, W:4 * W:3 * W - 1], in1=T.halo[:, 1:3], op=mult).then_inc(S.vi, 1)
+    V.wait_ge(S.vh, 1)
+    V.tensor_tensor(out=T.ys[:, 0:H], in0=T.ys[:, 0:H], in1=T.q[:, 0:2], op=add).then_inc(S.vj, 1)
+    V.tensor_tensor(out=T.ys[:, W - H:W], in0=T.ys[:, W - H:W], in1=T.q[:, 2:4], op=add).then_inc(S.vj, 1)
+    V.wait_ge(S.vi, 1)
+    V.wait_ge(S.vj, 2)
+    V.tensor_tensor(out=T.ys[:, 0:W:W - 1], in0=T.ys[:, 0:W:W - 1], in1=T.q[:, 4:6], op=add).then_inc(S.vdone, 1)
+
+    g.sync.wait_ge(S.vdone, 1)
+    g.sync.dma_start(T.y[:], T.ys[:]).then_inc(S.stored, 16)
+    g.sync.wait_ge(S.stored, 16)

@@ -7,7 +7,6 @@ H = 2
 
 SCRATCH = {
     "edge": ("dram", [2, 128, H], "float32"),
-    "land": ("dram", [2, 128, H], "float32"),
     "halo": ("sbuf", [128, 2 * H], "float32"),
     "xs": ("sbuf", [128, W], "float32"),
     "ts": ("sbuf", [128, KW * W], "float32"),
@@ -20,8 +19,11 @@ SCRATCH = {
     "te": ("sbuf", [128, 2 * H], "float32"),
     "q": ("sbuf", [128, 8], "float32"),
 }
-SEMAPHORES = ["cut", "xl", "tl", "relay", "sent", "arr0", "arr1", "hl", "vz", "vm", "va", "vg", "vh", "vi", "vj",
-              "vdone", "stored"]
+SEMAPHORES = ["cut", "xl", "tl", "relay", "sent", "arr", "vz", "vm", "va", "vg", "vh", "vi", "vj", "vdone", "stored"]
+
+
+def _count(mask):
+    return bin(mask).count("1")
 
 
 def _engines(allowed, n, busy=0):
@@ -58,16 +60,18 @@ def _plan(T, topo):
 def rank_program(g, core, T, topo):
     S = T.sem
     ways = _plan(T, topo)
-    arr = (S.arr0, S.arr1)
+
+    def deliver(slot, dst):
+        rid, pid = topo.addr(dst, core)
+        m = topo.mask(core, dst)
+        g.remote_dma(T.halo[:, H * slot:H * slot + H], T.edge[slot], S.arr, S.sent, pid, rid, m)
+        return _count(m)
 
     if T.rank_of(core) is None:
         for (src, slot, dst, via) in ways:
             if via == core:
-                rid, pid = topo.addr(dst, core)
                 g.wait_ge(S.relay, 1)
-                g.remote_dma(T.land[slot], T.edge[slot], arr[slot], S.sent, pid, rid,
-                             _engines(topo.mask(core, dst), 1))
-                g.wait_ge(S.sent, 1)
+                g.wait_ge(S.sent, deliver(slot, dst))
         return
 
     V, mult, add = g.vector, AluOpType.mult, AluOpType.add
@@ -87,18 +91,12 @@ def rank_program(g, core, T, topo):
             busy |= m
             trs.append(RemoteDMATransfer(dst_ids=[DstId(rid=rid, pnc=pid)], dma_engine_mask=m, remote_sem=S.relay,
                                          src=T.edge[slot], dst=T.edge[slot]))
-    if trs:
-        g.remote_dma_fused(trs, local_sem=S.sent)
+    left = len(trs)
+    g.remote_dma_fused(trs, local_sem=S.sent)
     for (src, slot, dst, via) in mine:
         if via is None:
-            rid, pid = topo.addr(dst, core)
-            g.remote_dma(T.land[slot], T.edge[slot], arr[slot], S.sent, pid, rid, _engines(topo.mask(core, dst), 1))
-    g.wait_ge(S.sent, len(mine))
-
-    g.sync.wait_ge(S.arr0, 1)
-    g.sync.dma_start(T.halo[:, 0:H], T.land[0]).then_inc(S.hl, 16)
-    g.scalar.wait_ge(S.arr1, 1)
-    g.scalar.dma_start(T.halo[:, H:2 * H], T.land[1]).then_inc(S.hl, 16)
+            left += deliver(slot, dst)
+    g.wait_ge(S.sent, left)
 
     V.memset(T.xz[:, 0:H], 0.0).then_inc(S.vz, 1)
     V.memset(T.xz[:, W + H:W + 2 * H], 0.0).then_inc(S.vz, 1)
@@ -120,7 +118,8 @@ def rank_program(g, core, T, topo):
     V.wait_ge(S.va, 3)
     V.wait_ge(S.vg, 2)
 
-    V.wait_ge(S.hl, 32)
+    V.wait_ge(S.arr, sum(_count(topo.mask(src if via is None else via, dst))
+                         for (src, slot, dst, via) in ways if dst == core))
     V.tensor_tensor(out=T.q[:, 0:4], in0=T.te[:], in1=T.halo[:], op=mult).then_inc(S.vh, 1)
     V.tensor_tensor(out=T.q[:, 4:6], in0=T.ts[:, W:4 * W:3 * W - 1], in1=T.halo[:, 1:3], op=mult).then_inc(S.vi, 1)
     V.wait_ge(S.vh, 1)

@@ -1,5 +1,5 @@
 from concourse.bass import DstId, RemoteDMATransfer
-from concourse.mybir import AluOpType
+from concourse.mybir import AluOpType, ActivationFunctionType
 
 W = 128
 KW = 5
@@ -16,10 +16,12 @@ SCRATCH = {
     "pc": ("sbuf", [128, W], "float32"),
     "u": ("sbuf", [128, W], "float32"),
     "ys": ("sbuf", [128, W], "float32"),
-    "te": ("sbuf", [128, 2 * H], "float32"),
-    "q": ("sbuf", [128, 8], "float32"),
+    "eb": ("sbuf", [128, 2 * H], "float32"),
+    "zl": ("sbuf", [128, 1], "float32"),
+    "zr": ("sbuf", [128, 1], "float32"),
 }
-SEMAPHORES = ["cut", "xl", "tl", "relay", "sent", "arr", "vz", "vm", "va", "vg", "vh", "vi", "vj", "vdone", "stored"]
+SEMAPHORES = ["cuta", "cutb", "xl", "tl", "relay", "sent", "arrl", "arrr", "vz", "vm", "va", "vg", "vh", "ah",
+              "vdone", "adone", "stored"]
 
 
 def _count(mask):
@@ -64,7 +66,7 @@ def rank_program(g, core, T, topo):
     def deliver(slot, dst):
         rid, pid = topo.addr(dst, core)
         m = topo.mask(core, dst)
-        g.remote_dma(T.halo[:, H * slot:H * slot + H], T.edge[slot], S.arr, S.sent, pid, rid, m)
+        g.remote_dma(T.halo[:, H * slot:H * slot + H], T.edge[slot], S.arrr if slot else S.arrl, S.sent, pid, rid, m)
         return _count(m)
 
     if T.rank_of(core) is None:
@@ -74,28 +76,27 @@ def rank_program(g, core, T, topo):
                 g.wait_ge(S.sent, deliver(slot, dst))
         return
 
-    V, mult, add = g.vector, AluOpType.mult, AluOpType.add
+    V, A, mult, add = g.vector, g.scalar, AluOpType.mult, AluOpType.add
+    ident = ActivationFunctionType.Identity
 
-    g.sync.dma_start(T.edge[0], T.x[:, W - H:W]).then_inc(S.cut, 16)
-    g.scalar.dma_start(T.edge[1], T.x[:, 0:H]).then_inc(S.cut, 16)
-    g.scalar.dma_start(T.xs[:], T.x[:]).then_inc(S.xl, 16)
+    mine = sorted((w for w in ways if w[0] == core), key=lambda w: w[3] is None)
+    cut = (S.cuta, S.cutb)
+    for k, (src, slot, dst, via) in enumerate(mine):
+        g.sync.dma_start(T.edge[slot], T.x[:, W - H:W] if slot == 0 else T.x[:, 0:H]).then_inc(cut[k], 16)
+    g.sync.dma_start(T.xs[:], T.x[:]).then_inc(S.xl, 16)
     g.sync.dma_start(T.ts[:], T.t[:]).then_inc(S.tl, 16)
 
-    mine = [w for w in ways if w[0] == core]
-    g.wait_ge(S.cut, 32)
-    busy, trs = 0, []
-    for (src, slot, dst, via) in mine:
-        if via is not None:
+    busy, left = 0, 0
+    for k, (src, slot, dst, via) in enumerate(mine):
+        g.wait_ge(cut[k], 16)
+        if via is None:
+            left += deliver(slot, dst)
+        else:
             rid, pid = topo.addr(via, core)
             m = _engines(topo.mask(core, via), 1, busy)
             busy |= m
-            trs.append(RemoteDMATransfer(dst_ids=[DstId(rid=rid, pnc=pid)], dma_engine_mask=m, remote_sem=S.relay,
-                                         src=T.edge[slot], dst=T.edge[slot]))
-    left = len(trs)
-    g.remote_dma_fused(trs, local_sem=S.sent)
-    for (src, slot, dst, via) in mine:
-        if via is None:
-            left += deliver(slot, dst)
+            g.remote_dma(T.edge[slot], T.edge[slot], S.relay, S.sent, pid, rid, m)
+            left += _count(m)
     g.wait_ge(S.sent, left)
 
     V.memset(T.xz[:, 0:H], 0.0).then_inc(S.vz, 1)
@@ -103,8 +104,6 @@ def rank_program(g, core, T, topo):
     V.wait_ge(S.xl, 16)
     V.tensor_copy(T.xz[:, H:W + H], T.xs[:]).then_inc(S.vz, 1)
     V.wait_ge(S.tl, 16)
-    V.tensor_copy(T.te[:, 0:H], T.ts[:, 0:H]).then_inc(S.vg, 1)
-    V.tensor_copy(T.te[:, H:2 * H], T.ts[:, KW * W - H:KW * W]).then_inc(S.vg, 1)
     V.wait_ge(S.vz, 3)
     outs = (T.pa[:, 0:W], T.pa[:, W:2 * W], T.pb[:, 0:W], T.pb[:, W:2 * W], T.pc[:])
     for i in range(KW):
@@ -116,19 +115,35 @@ def rank_program(g, core, T, topo):
     V.wait_ge(S.va, 2)
     V.tensor_tensor(out=T.ys[:], in0=T.pa[:, W:2 * W], in1=T.u[:], op=add).then_inc(S.va, 1)
     V.wait_ge(S.va, 3)
+    V.tensor_copy(T.eb[:, 0:H], T.ys[:, 0:H]).then_inc(S.vg, 1)
+    V.tensor_copy(T.eb[:, H:2 * H], T.ys[:, W - H:W]).then_inc(S.vg, 1)
     V.wait_ge(S.vg, 2)
 
-    V.wait_ge(S.arr, sum(_count(topo.mask(src if via is None else via, dst))
-                         for (src, slot, dst, via) in ways if dst == core))
-    V.tensor_tensor(out=T.q[:, 0:4], in0=T.te[:], in1=T.halo[:], op=mult).then_inc(S.vh, 1)
-    V.tensor_tensor(out=T.q[:, 4:6], in0=T.ts[:, W:4 * W:3 * W - 1], in1=T.halo[:, 1:3], op=mult).then_inc(S.vi, 1)
-    V.wait_ge(S.vh, 1)
-    V.tensor_tensor(out=T.ys[:, 0:H], in0=T.ys[:, 0:H], in1=T.q[:, 0:2], op=add).then_inc(S.vj, 1)
-    V.tensor_tensor(out=T.ys[:, W - H:W], in0=T.ys[:, W - H:W], in1=T.q[:, 2:4], op=add).then_inc(S.vj, 1)
-    V.wait_ge(S.vi, 1)
-    V.wait_ge(S.vj, 2)
-    V.tensor_tensor(out=T.ys[:, 0:W:W - 1], in0=T.ys[:, 0:W:W - 1], in1=T.q[:, 4:6], op=add).then_inc(S.vdone, 1)
+    def landed(slot):
+        return sum(_count(topo.mask(src if via is None else via, dst))
+                   for (src, sl, dst, via) in ways if dst == core and sl == slot)
 
-    g.sync.wait_ge(S.vdone, 1)
+    V.wait_ge(S.arrl, landed(0))
+    V.tensor_scalar(out=T.zl[:], in0=T.ts[:, 0:1], scalar1=T.halo[:, 0:1], scalar2=T.eb[:, 0:1],
+                    op0=mult, op1=add).then_inc(S.vh, 1)
+    V.tensor_scalar(out=T.ys[:, 1:2], in0=T.ts[:, 1:2], scalar1=T.halo[:, 1:2], scalar2=T.eb[:, 1:2],
+                    op0=mult, op1=add).then_inc(S.vdone, 1)
+    V.wait_ge(S.vh, 1)
+    V.tensor_scalar(out=T.ys[:, 0:1], in0=T.ts[:, W:W + 1], scalar1=T.halo[:, 1:2], scalar2=T.zl[:],
+                    op0=mult, op1=add).then_inc(S.vdone, 1)
+
+    A.wait_ge(S.tl, 16)
+    A.wait_ge(S.vg, 2)
+    A.wait_ge(S.arrr, landed(1))
+    A.activation(out=T.zr[:], in_=T.ts[:, KW * W - 1:KW * W], func=ident,
+                 bias=T.eb[:, 3:4], scale=T.halo[:, 3:4]).then_inc(S.ah, 1)
+    A.activation(out=T.ys[:, W - 2:W - 1], in_=T.ts[:, KW * W - 2:KW * W - 1], func=ident,
+                 bias=T.eb[:, 2:3], scale=T.halo[:, 2:3]).then_inc(S.adone, 1)
+    A.wait_ge(S.ah, 1)
+    A.activation(out=T.ys[:, W - 1:W], in_=T.ts[:, (KW - 1) * W - 1:(KW - 1) * W], func=ident,
+                 bias=T.zr[:], scale=T.halo[:, 2:3]).then_inc(S.adone, 1)
+
+    g.sync.wait_ge(S.vdone, 2)
+    g.sync.wait_ge(S.adone, 2)
     g.sync.dma_start(T.y[:], T.ys[:]).then_inc(S.stored, 16)
     g.sync.wait_ge(S.stored, 16)

from concourse.bass import DstId, RemoteDMATransfer
from concourse.mybir import AluOpType, ActivationFunctionType

W = 128
KW = 5
H = 2

SCRATCH = {
    "edge": ("dram", [2, 128, H], "float32"),
    "halo": ("sbuf", [128, 2 * H], "float32"),
    "xs": ("sbuf", [128, W], "float32"),
    "ts": ("sbuf", [128, KW * W], "float32"),
    "xz": ("psum", [128, W + 2 * H], "float32"),
    "pa": ("psum", [128, 2 * W], "float32"),
    "pb": ("sbuf", [128, 2 * W], "float32"),
    "pc": ("sbuf", [128, W], "float32"),
    "u": ("sbuf", [128, W], "float32"),
    "ys": ("sbuf", [128, W], "float32"),
    "eb": ("sbuf", [128, 2 * H], "float32"),
    "zl": ("sbuf", [128, 1], "float32"),
    "zr": ("sbuf", [128, 1], "float32"),
}
SEMAPHORES = ["cuta", "cutb", "xl", "tl", "relay", "sent", "arrl", "arrr", "vz", "vm", "va", "vg", "vh", "ah",
              "vdone", "adone", "stored"]


def _count(mask):
    return bin(mask).count("1")


def _engines(allowed, n, busy=0):
    m, bit = 0, 1
    while n:
        if allowed & bit and not busy & bit:
            m |= bit
            n -= 1
        bit <<= 1
    return m


def _plan(T, topo):
    cores = list(T.cores)
    n = len(cores)
    world = range((max(topo.host(c) for c in cores) + 1) * topo.CORES_PER_HOST)
    ways = []
    for r, c in enumerate(cores):
        taken = []
        for slot, step in ((0, 1), (1, -1)):
            dst = cores[(r + step) % n]
            via = None
            if not topo.may_write(c, dst):
                cand = [k for k in world
                        if topo.host(k) == topo.host(c) and topo.chip(k) == topo.chip(c) and k not in cores
                        and k not in taken and topo.may_write(k, dst)]
                cand.sort(key=lambda k: (topo.die(k) != topo.die(c), k))
                via = cand[0]
                taken.append(via)
            ways.append((c, slot, dst, via))
    return ways


def rank_program(g, core, T, topo):
    S = T.sem
    ways = _plan(T, topo)

    def deliver(slot, dst):
        rid, pid = topo.addr(dst, core)
        m = topo.mask(core, dst)
        g.remote_dma(T.halo[:, H * slot:H * slot + H], T.edge[slot], S.arrr if slot else S.arrl, S.sent, pid, rid, m)
        return _count(m)

    if T.rank_of(core) is None:
        for (src, slot, dst, via) in ways:
            if via == core:
                g.wait_ge(S.relay, 1)
                g.wait_ge(S.sent, deliver(slot, dst))
        return

    V, A, mult, add = g.vector, g.scalar, AluOpType.mult, AluOpType.add
    ident = ActivationFunctionType.Identity

    mine = sorted((w for w in ways if w[0] == core), key=lambda w: w[3] is None)
    cut = (S.cuta, S.cutb)
    for k, (src, slot, dst, via) in enumerate(mine):
        g.sync.dma_start(T.edge[slot], T.x[:, W - H:W] if slot == 0 else T.x[:, 0:H]).then_inc(cut[k], 16)
    g.sync.dma_start(T.xs[:], T.x[:]).then_inc(S.xl, 16)
    g.sync.dma_start(T.ts[:], T.t[:]).then_inc(S.tl, 16)

    busy, left = 0, 0
    for k, (src, slot, dst, via) in enumerate(mine):
        g.wait_ge(cut[k], 16)
        if via is None:
            left += deliver(slot, dst)
        else:
            rid, pid = topo.addr(via, core)
            m = _engines(topo.mask(core, via), 1, busy)
            busy |= m
            g.remote_dma(T.edge[slot], T.edge[slot], S.relay, S.sent, pid, rid, m)
            left += _count(m)
    g.wait_ge(S.sent, left)

    V.memset(T.xz[:, 0:H], 0.0).then_inc(S.vz, 1)
    V.memset(T.xz[:, W + H:W + 2 * H], 0.0).then_inc(S.vz, 1)
    V.wait_ge(S.xl, 16)
    V.tensor_copy(T.xz[:, H:W + H], T.xs[:]).then_inc(S.vz, 1)
    V.wait_ge(S.tl, 16)
    V.wait_ge(S.vz, 3)
    outs = (T.pa[:, 0:W], T.pa[:, W:2 * W], T.pb[:, 0:W], T.pb[:, W:2 * W], T.pc[:])
    for i in range(KW):
        V.tensor_tensor(out=outs[i], in0=T.ts[:, W * i:W * i + W], in1=T.xz[:, i:i + W], op=mult).then_inc(S.vm, 1)
    V.wait_ge(S.vm, KW)
    V.tensor_tensor(out=T.pa[:], in0=T.pa[:], in1=T.pb[:], op=add).then_inc(S.va, 1)
    V.wait_ge(S.va, 1)
    V.tensor_tensor(out=T.u[:], in0=T.pa[:, 0:W], in1=T.pc[:], op=add).then_inc(S.va, 1)
    V.wait_ge(S.va, 2)
    V.tensor_tensor(out=T.ys[:], in0=T.pa[:, W:2 * W], in1=T.u[:], op=add).then_inc(S.va, 1)
    V.wait_ge(S.va, 3)
    V.tensor_copy(T.eb[:, 0:H], T.ys[:, 0:H]).then_inc(S.vg, 1)
    V.tensor_copy(T.eb[:, H:2 * H], T.ys[:, W - H:W]).then_inc(S.vg, 1)
    V.wait_ge(S.vg, 2)

    def landed(slot):
        return sum(_count(topo.mask(src if via is None else via, dst))
                   for (src, sl, dst, via) in ways if dst == core and sl == slot)

    V.wait_ge(S.arrl, landed(0))
    V.tensor_scalar(out=T.zl[:], in0=T.ts[:, 0:1], scalar1=T.halo[:, 0:1], scalar2=T.eb[:, 0:1],
                    op0=mult, op1=add).then_inc(S.vh, 1)
    V.tensor_scalar(out=T.ys[:, 1:2], in0=T.ts[:, 1:2], scalar1=T.halo[:, 1:2], scalar2=T.eb[:, 1:2],
                    op0=mult, op1=add).then_inc(S.vdone, 1)
    V.wait_ge(S.vh, 1)
    V.tensor_scalar(out=T.ys[:, 0:1], in0=T.ts[:, W:W + 1], scalar1=T.halo[:, 1:2], scalar2=T.zl[:],
                    op0=mult, op1=add).then_inc(S.vdone, 1)

    A.wait_ge(S.tl, 16)
    A.wait_ge(S.vg, 2)
    A.wait_ge(S.arrr, landed(1))
    A.activation(out=T.zr[:], in_=T.ts[:, KW * W - 1:KW * W], func=ident,
                 bias=T.eb[:, 3:4], scale=T.halo[:, 3:4]).then_inc(S.ah, 1)
    A.activation(out=T.ys[:, W - 2:W - 1], in_=T.ts[:, KW * W - 2:KW * W - 1], func=ident,
                 bias=T.eb[:, 2:3], scale=T.halo[:, 2:3]).then_inc(S.adone, 1)
    A.wait_ge(S.ah, 1)
    A.activation(out=T.ys[:, W - 1:W], in_=T.ts[:, (KW - 1) * W - 1:(KW - 1) * W], func=ident,
                 bias=T.zr[:], scale=T.halo[:, 2:3]).then_inc(S.adone, 1)

    g.sync.wait_ge(S.vdone, 2)
    g.sync.wait_ge(S.adone, 2)
    g.sync.dma_start(T.y[:], T.ys[:]).then_inc(S.stored, 16)
    g.sync.wait_ge(S.stored, 16)
